import numpy as np
import ml_dtypes

BF16 = ml_dtypes.bfloat16


def bf(x):
    return np.asarray(x, np.float32).astype(BF16)


def f32(x):
    return np.asarray(x, np.float32)


def f64(x):
    return np.asarray(x).astype(np.float64)


def striped(idx):
    return np.tile(idx.reshape(-1, 16).T, (8, 1))


S, K, M, N, D, V = 512, 256, 128, 384, 4, 96


def setup_inputs():
    return {"table": bf(np.random.standard_normal((K, S))), "w": bf(np.random.standard_normal((K, M)) / np.sqrt(D * K)), "r": f32(np.random.standard_normal((M, V))), "offs": striped(np.random.permutation(np.tile(np.arange(S), 2))[:N])}


def reference(table, w, r, offs):
    idx = offs[:16].T.reshape(-1)
    x = f64(table)[:, idx]
    y = f64(w).T @ sum(x[:, t * V : (t + 1) * V] for t in range(D))
    return y + f64(r)

@@ -1,0 +1,50 @@
+import concourse.mybir as mybir
+
+BF16, F32, U16 = mybir.dt.bfloat16, mybir.dt.float32, mybir.dt.uint16
+
+P = 128
+K = 256
+S = 512
+M = 128
+V = 96
+D = 4
+N = D * V
+KB = K // P
+PIECE_COLS = V // 16
+
+FLOPS = 2 * K * M * N
+
+
+def tile_gather_matmul_kernel(tc, table, w, r, offs, out):
+    nc = tc.nc
+    with (
+        tc.tile_pool(name="held", bufs=1) as held,
+        tc.psum_pool(name="psum", bufs=1) as psum,
+    ):
+        offsets = held.tile([P, N // 16], U16, name="offsets")
+        nc.sync.dma_start(offsets[:], offs)
+
+        blocks = [held.tile([P, S], BF16, name=f"block{b}") for b in range(KB)]
+        weights = [held.tile([P, M], BF16, name=f"weights{b}") for b in range(KB)]
+        own = held.tile([M, V], F32, name="own")
+        nc.scalar.dma_start(weights[0][:], w[0:P, :])
+        nc.sync.dma_start(blocks[0][:], table[0:P, :])
+        nc.scalar.dma_start(blocks[1][:], table[P : 2 * P, :])
+        nc.sync.dma_start(weights[1][:], w[P : 2 * P, :])
+        nc.gpsimd.dma_start(own[:], r)
+
+        y = psum.tile([M, V], F32, name="y")
+        for b in range(KB):
+            for t in range(D):
+                piece = offsets[:, t * PIECE_COLS : (t + 1) * PIECE_COLS]
+                nc.tensor.matmul(
+                    y[:],
+                    weights[b][:],
+                    blocks[b][:].indirect(piece),
+                    start=(b == 0 and t == 0),
+                    stop=(b == KB - 1 and t == D - 1),
+                )
+
+        result = held.tile([M, V], F32, name="result")
+        nc.vector.tensor_tensor(result[:], y[:], own[:], mybir.AluOpType.add)
+        nc.sync.dma_start(out, result[:])

@@ -25,13 +25,13 @@ def tile_gather_matmul_kernel(tc, table, w, r, offs, out):
         nc.sync.dma_start(offsets[:], offs)
 
         blocks = [held.tile([P, S], BF16, name=f"block{b}") for b in range(KB)]
-        weights = [held.tile([P, M], BF16, name=f"weights{b}") for b in range(KB)]
+        for b in range(KB):
+            nc.sync.dma_start(blocks[b][:], table[b * P : (b + 1) * P, :])
+
+        weights = held.tile([P, KB, M], BF16, name="weights")
+        nc.scalar.dma_start(weights[:], w.rearrange("(b p) m -> p b m", p=P))
         own = held.tile([M, V], F32, name="own")
-        nc.scalar.dma_start(weights[0][:], w[0:P, :])
-        nc.sync.dma_start(blocks[0][:], table[0:P, :])
-        nc.scalar.dma_start(blocks[1][:], table[P : 2 * P, :])
-        nc.sync.dma_start(weights[1][:], w[P : 2 * P, :])
-        nc.gpsimd.dma_start(own[:], r)
+        nc.scalar.dma_start(own[:], r)
 
         y = psum.tile([M, V], F32, name="y")
         for b in range(KB):
@@ -39,7 +39,7 @@ def tile_gather_matmul_kernel(tc, table, w, r, offs, out):
                 piece = offsets[:, t * PIECE_COLS : (t + 1) * PIECE_COLS]
                 nc.tensor.matmul(
                     y[:],
-                    weights[b][:],
+                    weights[:, b, :],
                     blocks[b][:].indirect(piece),
                     start=(b == 0 and t == 0),
                     stop=(b == KB - 1 and t == D - 1),

@@ -15,6 +15,9 @@ PIECE_COLS = V // 16
 FLOPS = 2 * K * M * N
 
 
+WARM_UPS = 16
+
+
 def tile_gather_matmul_kernel(tc, table, w, r, offs, out):
     nc = tc.nc
     with (
@@ -32,6 +35,12 @@ def tile_gather_matmul_kernel(tc, table, w, r, offs, out):
         nc.scalar.dma_start(weights[:], w.rearrange("(b p) m -> p b m", p=P))
         own = held.tile([M, V], F32, name="own")
         nc.scalar.dma_start(own[:], r)
+
+        zeros = held.tile([P, P], BF16, name="zeros")
+        nc.vector.memset(zeros[:], 0.0)
+        idle = psum.tile([P, P], F32, name="idle")
+        for i in range(WARM_UPS):
+            nc.tensor.matmul(idle[:], zeros[:], zeros[:], start=True, stop=True)
 
         y = psum.tile([M, V], F32, name="y")
         for b in range(KB):

@@ -15,7 +15,8 @@ PIECE_COLS = V // 16
 FLOPS = 2 * K * M * N
 
 
-WARM_UPS = 16
+QUARTER = 32
+WARM_ROUNDS = 3
 
 
 def tile_gather_matmul_kernel(tc, table, w, r, offs, out):
@@ -38,9 +39,11 @@ def tile_gather_matmul_kernel(tc, table, w, r, offs, out):
 
         zeros = held.tile([P, P], BF16, name="zeros")
         nc.vector.memset(zeros[:], 0.0)
-        idle = psum.tile([P, P], F32, name="idle")
-        for i in range(WARM_UPS):
-            nc.tensor.matmul(idle[:], zeros[:], zeros[:], start=True, stop=True)
+        idle = psum.tile([P, 4, P], F32, name="idle")
+        many = zeros[:].unsqueeze(1).to_broadcast([P, 4, P])
+        for i in range(WARM_ROUNDS):
+            for q in range(0, P, QUARTER):
+                nc.tensor.matmul(idle[q : q + QUARTER], zeros[:, :QUARTER], many, start=True, stop=True)
 
         y = psum.tile([M, V], F32, name="y")
         for b in range(KB):

@@ -28,12 +28,13 @@ def tile_gather_matmul_kernel(tc, table, w, r, offs, out):
         offsets = held.tile([P, N // 16], U16, name="offsets")
         nc.sync.dma_start(offsets[:], offs)
 
+        interleaved = table.rearrange("(p b) s -> b p s", b=KB)
         blocks = [held.tile([P, S], BF16, name=f"block{b}") for b in range(KB)]
         for b in range(KB):
-            nc.sync.dma_start(blocks[b][:], table[b * P : (b + 1) * P, :])
+            nc.sync.dma_start(blocks[b][:], interleaved[b])
 
         weights = held.tile([P, KB, M], BF16, name="weights")
-        nc.scalar.dma_start(weights[:], w.rearrange("(b p) m -> p b m", p=P))
+        nc.scalar.dma_start(weights[:], w.rearrange("(p b) m -> p b m", b=KB))
         own = held.tile([M, V], F32, name="own")
         nc.scalar.dma_start(own[:], r)
 

@@ -25,16 +25,15 @@ def tile_gather_matmul_kernel(tc, table, w, r, offs, out):
         tc.tile_pool(name="held", bufs=1) as held,
         tc.psum_pool(name="psum", bufs=1) as psum,
     ):
-        offsets = held.tile([P, N // 16], U16, name="offsets")
-        nc.sync.dma_start(offsets[:], offs)
-
         interleaved = table.rearrange("(p b) s -> b p s", b=KB)
         blocks = [held.tile([P, S], BF16, name=f"block{b}") for b in range(KB)]
-        for b in range(KB):
-            nc.sync.dma_start(blocks[b][:], interleaved[b])
-
+        offsets = held.tile([P, N // 16], U16, name="offsets")
         weights = held.tile([P, KB, M], BF16, name="weights")
-        nc.scalar.dma_start(weights[:], w.rearrange("(p b) m -> p b m", b=KB))
+        nc.sync.dma_start(blocks[0][:], interleaved[0])
+        nc.sync.dma_start(offsets[:], offs)
+        nc.sync.dma_start(weights[:], w.rearrange("(p b) m -> p b m", b=KB))
+        nc.sync.dma_start(blocks[1][:], interleaved[1])
+
         own = held.tile([M, V], F32, name="own")
         nc.scalar.dma_start(own[:], r)
 

@@ -35,7 +35,7 @@ def tile_gather_matmul_kernel(tc, table, w, r, offs, out):
         nc.sync.dma_start(blocks[1][:], interleaved[1])
 
         own = held.tile([M, V], F32, name="own")
-        nc.scalar.dma_start(own[:], r)
+        nc.sync.dma_start(own[:], r)
 
         zeros = held.tile([P, P], BF16, name="zeros")
         nc.vector.memset(zeros[:], 0.0)

@@ -16,7 +16,7 @@ FLOPS = 2 * K * M * N
 
 
 QUARTER = 32
-WARM_ROUNDS = 3
+WARM_ROUNDS = 2
 
 
 def tile_gather_matmul_kernel(tc, table, w, r, offs, out):

import concourse.mybir as mybir

BF16, F32, U16 = mybir.dt.bfloat16, mybir.dt.float32, mybir.dt.uint16

P = 128
K = 256
S = 512
M = 128
V = 96
D = 4
N = D * V
KB = K // P
PIECE_COLS = V // 16

FLOPS = 2 * K * M * N


QUARTER = 32
WARM_ROUNDS = 2


def tile_gather_matmul_kernel(tc, table, w, r, offs, out):
    nc = tc.nc
    with (
        tc.tile_pool(name="held", bufs=1) as held,
        tc.psum_pool(name="psum", bufs=1) as psum,
    ):
        interleaved = table.rearrange("(p b) s -> b p s", b=KB)
        blocks = [held.tile([P, S], BF16, name=f"block{b}") for b in range(KB)]
        offsets = held.tile([P, N // 16], U16, name="offsets")
        weights = held.tile([P, KB, M], BF16, name="weights")
        nc.sync.dma_start(blocks[0][:], interleaved[0])
        nc.sync.dma_start(offsets[:], offs)
        nc.sync.dma_start(weights[:], w.rearrange("(p b) m -> p b m", b=KB))
        nc.sync.dma_start(blocks[1][:], interleaved[1])

        own = held.tile([M, V], F32, name="own")
        nc.sync.dma_start(own[:], r)

        zeros = held.tile([P, P], BF16, name="zeros")
        nc.vector.memset(zeros[:], 0.0)
        idle = psum.tile([P, 4, P], F32, name="idle")
        many = zeros[:].unsqueeze(1).to_broadcast([P, 4, P])
        for i in range(WARM_ROUNDS):
            for q in range(0, P, QUARTER):
                nc.tensor.matmul(idle[q : q + QUARTER], zeros[:, :QUARTER], many, start=True, stop=True)

        y = psum.tile([M, V], F32, name="y")
        for b in range(KB):
            for t in range(D):
                piece = offsets[:, t * PIECE_COLS : (t + 1) * PIECE_COLS]
                nc.tensor.matmul(
                    y[:],
                    weights[:, b, :],
                    blocks[b][:].indirect(piece),
                    start=(b == 0 and t == 0),
                    stop=(b == KB - 1 and t == D - 1),
                )

        result = held.tile([M, V], F32, name="result")
        nc.vector.tensor_tensor(result[:], y[:], own[:], mybir.AluOpType.add)
        nc.sync.dma_start(out, result[:])
